import numpy as np
import ml_dtypes


def mxq(x, axis, fmt="e4m3"):
    dtype, down = {"e4m3": (ml_dtypes.float8_e4m3fn, 7), "e5m2": (ml_dtypes.float8_e5m2, 14)}[fmt]
    v = np.moveaxis(np.asarray(x, np.float32).astype(ml_dtypes.bfloat16).astype(np.float64), axis, -1)
    blocks = v.reshape(v.shape[:-1] + (-1, 32))
    amax = np.abs(blocks).max(-1, keepdims=True)
    byte = np.maximum(np.where(amax > 0, np.frexp(amax)[1] - 1 + 127, 0) - down, 1)
    scale = np.exp2(byte - 127.0)
    codes = (blocks / scale).astype(np.float32).astype(dtype).astype(np.float64)
    return np.moveaxis((codes * scale).reshape(v.shape), -1, axis)


WIDE = False


def mx_kscale(k):
    if not WIDE:
        return np.ones(k)
    levels = np.array([10, -10, 5, -5, 0])
    if k % 512:
        return np.exp2(np.random.permutation(np.resize(levels, k // 32))).repeat(32)
    a = np.empty((k // 512, 16))
    for p in range(k // 512):
        a[p, :8] = np.random.permutation(np.resize(levels, 8))
        for g in range(8):
            far = levels[np.abs(levels - a[p, g]) >= 10]
            a[p, g + 8] = far[np.random.randint(len(far))]
    return np.exp2(a.ravel()).repeat(32)


BF16 = ml_dtypes.bfloat16


def bf(x):
    return np.asarray(x, np.float32).astype(BF16)


def f64(x):
    return np.asarray(x).astype(np.float64)


E2M1 = np.array([0.0, 0.5, 1.0, 1.5, 2.0, 3.0, 4.0, 6.0, -0.0, -0.5, -1.0, -1.5, -2.0, -3.0, -4.0, -6.0])


def pack_weight(w, fmt):
    k, n = w.shape
    w = f64(bf(w)).reshape(k // 32, 32, n)
    amax = np.abs(w).max(1)
    if fmt == "e4m3":
        byte = np.frexp(amax)[1] - 1 + 127 - 7
    else:
        mant, ex = np.frexp(amax / 6.0)
        byte = np.where(mant > 0.5, ex, ex - 1) + 127
    byte = np.clip(np.where(amax > 0, byte, 1), 1, 254)
    scaled = (w * np.exp2(127.0 - byte)[:, None, :]).reshape(k, n).astype(np.float32)
    by_word = np.ascontiguousarray(scaled.reshape(k // 512, 128, 4, n).transpose(0, 1, 3, 2))
    if fmt == "e4m3":
        words = by_word.astype(ml_dtypes.float8_e4m3fn).view(np.uint8)
    else:
        c = by_word.astype(ml_dtypes.float4_e2m1fn).view(np.uint8) & 0xF
        words = c[..., 0::2] | (c[..., 1::2] << 4)
    return np.ascontiguousarray(words), np.ascontiguousarray(byte.astype(np.uint8).reshape(k // 512, 16, n))


def unpack_weight(words, scales, fmt):
    g, p, n, _ = words.shape
    if fmt == "e4m3":
        vals = np.ascontiguousarray(words).view(ml_dtypes.float8_e4m3fn).astype(np.float64)
    else:
        nib = np.empty((g, p, n, 4), np.uint8)
        nib[..., 0::2] = words & 0xF
        nib[..., 1::2] = words >> 4
        vals = E2M1[nib]
    vals = vals * np.repeat(np.exp2(scales.astype(np.float64) - 127.0), 8, axis=1)[..., None]
    return vals.transpose(0, 1, 3, 2).reshape(g * 512, n)
def pack4(w):
    words, scales = pack_weight(w, "e2m1")
    return words.reshape(words.shape[0], 128, -1), scales


def unpack4(words, scales):
    return unpack_weight(words.reshape(words.shape[0], 128, -1, 2), scales, "e2m1")


def planes(Y):
    n, m = Y.shape
    b = f64(bf(Y)).reshape(n // 32, 32, m)
    amax = np.abs(b).max(1)
    byte = np.clip(np.where(amax > 0, np.frexp(amax)[1] - 1 + 127 - 7, 1), 1, 254)
    codes = (b * np.exp2(127.0 - byte)[:, None, :]).reshape(n, m).astype(np.float32).astype(ml_dtypes.float8_e4m3fn).view(np.uint8)
    words = codes.reshape(n // 512, 128, 4, m).transpose(0, 1, 3, 2)
    return np.ascontiguousarray(words), np.ascontiguousarray(byte.astype(np.uint8).reshape(n // 512, 16, m))


M, K, R, N = 1024, 2048, 512, 1536
P_DROP = 0.2
LORA_SCALE = 2.0


def setup_inputs():
    s = mx_kscale(K)
    t = mx_kscale(R)
    spread = np.exp(0.8 * np.random.randn(N))
    x = np.random.randn(M, K) * s
    w0 = 0.7 * np.random.randn(K, N) / np.sqrt(K) * spread / s[:, None]
    a = np.random.randn(K, R) / np.sqrt(K) / s[:, None] * t
    b = 0.3 * np.random.randn(R, N) / np.sqrt(R) * spread / t[:, None]
    keep = np.random.rand(M, R) >= P_DROP
    w0_words, w0_scales = pack4(w0)
    a_words, a_scales = pack4(a)
    return {"x": bf(x), "w0_words": w0_words, "w0_scales": w0_scales,
            "a_words": a_words, "a_scales": a_scales,
            "drop": bf(keep / (1.0 - P_DROP)), "b": bf(b),
            "bias": bf(0.3 * np.random.randn(N) * spread),
            "residual": bf(0.5 * np.random.randn(M, N) * spread)}


def reference(x, w0_words, w0_scales, a_words, a_scales, drop, b, bias, residual):
    xq = mxq(f64(x), 1, "e4m3")
    w0 = unpack4(w0_words, w0_scales)
    a = unpack4(a_words, a_scales)
    h = (xq @ a) * f64(drop)
    delta = mxq(h, 1, "e4m3") @ mxq(f64(b), 0, "e4m3")
    base = xq @ w0
    y = base + LORA_SCALE * delta + f64(bias) + f64(residual)
    Y = y.T
    words, scales = planes(Y)
    return y, words, scales

@@ -1,0 +1,460 @@
+from contextlib import ExitStack
+
+import concourse.mybir as mybir
+from concourse.masks import make_identity
+
+M, K, R, N = 1024, 2048, 512, 1536
+LORA_SCALE = 2.0
+FLOPS = 2 * M * (K * R + K * N + R * N)
+
+F32 = mybir.dt.float32
+BF16 = mybir.dt.bfloat16
+I32 = mybir.dt.int32
+U32 = mybir.dt.uint32
+U8 = mybir.dt.uint8
+FP8X4 = mybir.dt.float8_e4m3fn_x4
+FP4X4 = mybir.dt.float4_e2m1fn_x4
+MULT = mybir.AluOpType.mult
+ADD = mybir.AluOpType.add
+
+P = 128
+PASS = 512
+PASSES = K // PASS
+TILES = M // P
+GROUPS = N // PASS
+HEAD = 3
+BLOCKS = [(0, 3), (3, 6), (6, 8)]
+
+
+def tile_lora_dropout_output_projection_h1_kernel(
+    tc, x, w0_words, w0_scales, a_words, a_scales, drop, b, bias, residual, out_0, out_1, out_2
+):
+    nc = tc.nc
+    with ExitStack() as ctx:
+        keep = ctx.enter_context(tc.tile_pool(name="keep", bufs=1))
+        stage = ctx.enter_context(tc.tile_pool(name="stage", bufs=2))
+        psum = ctx.enter_context(tc.psum_pool(name="psum", bufs=1))
+        ctx.enter_context(tc.manual_schedule())
+
+        def kept(name, shape, dtype):
+            return keep.tile(shape, dtype, name=name, align_bytes=64)
+
+        def staged(tag, shape, dtype, bufs):
+            return stage.tile(shape, dtype, name=tag, tag=tag, bufs=bufs, align_bytes=64)
+
+        turn = {"t": 0, "m": 0}
+
+        def bank(kind, shape):
+            tag = "%s%d" % (kind, turn[kind] % 4)
+            turn[kind] = turn[kind] + 1
+            return psum.tile(shape, F32, name=tag, tag=tag)
+
+        ident = kept("ident", [P, P], F32)
+        make_identity(nc, ident[:])
+        a_sc = kept("a_sc", [P, PASSES, R], U8)
+        w_sc_first = kept("w_sc_first", [P, PASSES, PASS], U8)
+        w_sc_rest = kept("w_sc_rest", [P, PASSES, N - PASS], U8)
+        for plane in (a_sc, w_sc_first, w_sc_rest):
+            nc.vector.memset(plane[:].bitcast(I32), 0)
+
+        x_half = {}
+        drop_sb = {}
+        res_sb = {}
+        w_sb = {}
+        b_sb = {}
+
+        def load_scales(plane, rows):
+            by_r = rows.rearrange("g (q r) n -> r q g n", r=4)
+            for r in range(4):
+                nc.sync.dma_start(out=plane[:].bitcast(I32)[r:P:32, :, :], in_=by_r[r])
+
+        def load_x(i):
+            rows = x[i * P:(i + 1) * P, :]
+            if i == 0:
+                for h in range(2):
+                    t = kept("x%d_%d" % (i, h), [P, K // 2], BF16)
+                    nc.sync.dma_start(out=t[:], in_=rows[:, h * (K // 2):(h + 1) * (K // 2)])
+                    x_half[(i, h)] = t[:].bitcast(F32)
+            else:
+                t = kept("x%d" % i, [P, K], BF16)
+                nc.sync.dma_start(out=t[:], in_=rows)
+                for h in range(2):
+                    x_half[(i, h)] = t[:].bitcast(F32)[:, h * (K // 4):(h + 1) * (K // 4)]
+                x_half[i] = t[:].bitcast(F32)
+
+        def load_drop(i):
+            t = kept("drop%d" % i, [P, R], BF16)
+            nc.sync.dma_start(out=t[:], in_=drop[i * P:(i + 1) * P, :])
+            drop_sb[i] = t
+
+        def load_w(c):
+            t = kept("w%d" % c, [P, PASSES, 2 * PASS], U8)
+            src = w0_words.bitcast(I32)[:, :, c * 256:(c + 1) * 256].rearrange("g p n -> p g n")
+            nc.sync.dma_start(out=t[:].bitcast(I32), in_=src)
+            w_sb[c] = t
+
+        def load_b(c):
+            t = kept("b%d" % c, [P, 4, PASS], BF16)
+            nc.sync.dma_start(out=t[:], in_=b[:, c * PASS:(c + 1) * PASS].rearrange("(p j) n -> p j n", j=4))
+            b_sb[c] = t
+
+        def load_res_head(c):
+            t = kept("resh%d" % c, [P, HEAD, PASS], BF16)
+            src = residual[0:HEAD * P, c * PASS:(c + 1) * PASS].rearrange("(i p) n -> p i n", p=P)
+            nc.sync.dma_start(out=t[:], in_=src)
+            for i in range(HEAD):
+                res_sb[(i, c)] = t[:, i, :]
+
+        def load_res(i):
+            t = kept("res%d" % i, [P, N], BF16)
+            nc.sync.dma_start(out=t[:], in_=residual[i * P:(i + 1) * P, :])
+            for c in range(GROUPS):
+                res_sb[(i, c)] = t[:, c * PASS:(c + 1) * PASS]
+
+        load_x(0)
+        bias_col = kept("bias_col", [P, GROUPS * 4], BF16)
+        nc.sync.dma_start(
+            out=bias_col[:].rearrange("p (c e) -> p c e", e=4),
+            in_=bias.rearrange("(c p e) -> p c e", p=P, e=4),
+        )
+        a_sb = kept("a_sb", [P, PASSES, 2 * R], U8)
+        nc.sync.dma_start(out=a_sb[:].bitcast(I32), in_=a_words.bitcast(I32).rearrange("g p n -> p g n"))
+        load_scales(a_sc, a_scales.bitcast(I32))
+        load_x(1)
+        load_drop(0)
+        load_x(2)
+        load_b(0)
+        load_drop(1)
+        load_w(0)
+        load_scales(w_sc_first, w0_scales.bitcast(I32)[:, :, 0:PASS // 4])
+        load_drop(2)
+        load_res_head(0)
+        load_b(1)
+        load_w(1)
+        load_scales(w_sc_rest, w0_scales.bitcast(I32)[:, :, PASS // 4:N // 4])
+        load_res_head(1)
+        load_x(3)
+        load_b(2)
+        load_w(2)
+        load_drop(3)
+        load_res_head(2)
+        for i in range(HEAD + 1, TILES):
+            load_x(i)
+            load_drop(i)
+            load_res(i - 1)
+        load_res(TILES - 1)
+
+        def w_scale(g, c):
+            if c == 0:
+                return w_sc_first[:, g, :]
+            return w_sc_rest[:, g, (c - 1) * PASS:c * PASS]
+
+        bias_bc = kept("bias_bc", [P, N], BF16)
+        xq = {}
+        hq = {}
+        bq = {}
+        x_sorted = {}
+        h_bank = {}
+        h_bf = {}
+        y_f32 = {}
+        y_bank = {}
+        y_bf = {}
+        words = {}
+        planes = {}
+        for first, last in BLOCKS:
+            width = (last - first) * P
+            plane = kept("ysc%d" % first, [P, GROUPS, width], U8)
+            for c in range(GROUPS):
+                codes = kept("yq%d_%d" % (first, c), [P, width], U32)
+                for i in range(first, last):
+                    words[(i, c)] = (codes, first, last)
+            for i in range(first, last):
+                planes[i] = plane
+
+        def sorted_out(ap):
+            return ap.rearrange("p (u q e) -> p u q e", u=2, e=2)
+
+        def sorted_in(ap):
+            return ap.rearrange("p (q u e) -> p u q e", u=2, e=2)
+
+        def transpose_pair(dst, slot, sources):
+            for u in range(2):
+                nc.tensor.transpose(dst[:, slot + u, :], sources[u], ident[:])
+
+        def word_halves(tile_bf):
+            w = tile_bf[:].bitcast(F32)
+            return [w[:, 0:P], w[:, P:2 * P]]
+
+        def copy_pair(dst_words, src, slot):
+            nc.scalar.copy(
+                out=dst_words.rearrange("p (r u) -> p r u", u=2),
+                in_=src[:, slot:slot + 2, :].rearrange("p u r -> p r u"),
+            )
+
+        def quantize(codes, scales, grouped):
+            nc.vector.quantize_mx(out=codes.bitcast(FP8X4), scales=scales, in_=grouped)
+
+        def sort_x(i):
+            t = staged("xs", [P, K // 2], F32, 2)
+            nc.scalar.copy(
+                out=t[:].rearrange("p (g u q) -> p g u q", u=2, q=P),
+                in_=x_half[i].rearrange("p (g q u) -> p g u q", u=2, q=P),
+            )
+            x_sorted[i] = t
+
+        def transpose_x(i):
+            banks = []
+            for h in range(2):
+                t = bank("t", [P, 4, P])
+                for g in range(2):
+                    if i in x_sorted:
+                        at = (2 * h + g) * 256
+                        src = [x_sorted[i][:, at:at + P], x_sorted[i][:, at + P:at + 2 * P]]
+                    else:
+                        src = [x_half[(i, h)][:, g * 256 + u:(g + 1) * 256:2] for u in range(2)]
+                    transpose_pair(t, 2 * g, src)
+                banks.append(t)
+            return banks
+
+        def finish_x(i, h, banks):
+            grouped = staged("xg", [P, K // 2], BF16, 3)
+            nc.scalar.copy(
+                out=grouped[:].bitcast(F32).rearrange("p (g r u) -> p g r u", g=2, u=2),
+                in_=banks[h][:].rearrange("p (g u) r -> p g r u", u=2),
+            )
+            codes = kept("xq%d_%d" % (i, h), [P, 2 * P], U32)
+            scales = kept("xsc%d_%d" % (i, h), [P, 2 * P], U8)
+            quantize(codes[:], scales[:], grouped[:])
+            for g in range(2):
+                xq[(i, 2 * h + g)] = (codes[:, g * P:(g + 1) * P], scales[:, g * P:(g + 1) * P])
+
+        b_grouped = {}
+
+        def b_views(c, h):
+            if c not in b_grouped:
+                b_grouped[c] = staged("bg", [P, 4 * PASS], BF16, 2)
+            dst = b_grouped[c][:, h * 2 * PASS:(h + 1) * 2 * PASS].rearrange("p (n i t) -> p n t i", i=4, t=4)
+            src = b_sb[c][:, :, h * 256:(h + 1) * 256].rearrange("p t (n i) -> p n t i", i=4)
+            return dst, src
+
+        def group_b_vector(c):
+            dst, src = b_views(c, 0)
+            nc.vector.tensor_scalar(out=dst, in0=src, scalar1=LORA_SCALE, scalar2=None, op0=MULT)
+
+        def group_b_scalar(c, h):
+            dst, src = b_views(c, h)
+            nc.scalar.activation(out=dst, in_=src, func=mybir.ActivationFunctionType.Copy, scale=LORA_SCALE)
+
+        def quantize_b(c):
+            grouped = b_grouped[c]
+            codes = kept("bq%d" % c, [P, PASS], U32)
+            scales = kept("bsc%d" % c, [P, PASS], U8)
+            quantize(codes[:], scales[:], grouped[:])
+            bq[c] = (codes, scales)
+
+        def multiply_h(i):
+            acc = bank("m", [P, R])
+            for g in range(PASSES):
+                codes, scales = xq[(i, g)]
+                nc.tensor.matmul_mx(
+                    out=acc[:], lhsT=codes.bitcast(FP8X4), lhsT_scale=scales,
+                    rhs=a_sb[:, g, :].bitcast(FP4X4), rhs_scale=a_sc[:, g, :],
+                    start=(g == 0), stop=(g == PASSES - 1),
+                )
+            h_bank[i] = acc
+
+        def drop_h(i):
+            t = staged("hbf", [P, R], BF16, 3)
+            nc.vector.tensor_tensor(
+                out=sorted_out(t[:]), in0=sorted_in(h_bank[i][:]), in1=sorted_in(drop_sb[i][:]), op=MULT
+            )
+            h_bf[i] = t
+
+        def multiply_y(unit):
+            i, c = unit
+            acc = bank("m", [P, PASS])
+            for g in range(PASSES):
+                codes, scales = xq[(i, g)]
+                nc.tensor.matmul_mx(
+                    out=acc[:], lhsT=codes.bitcast(FP8X4), lhsT_scale=scales,
+                    rhs=w_sb[c][:, g, :].bitcast(FP4X4), rhs_scale=w_scale(g, c),
+                    start=(g == 0), stop=False,
+                )
+            nc.tensor.matmul_mx(
+                out=acc[:], lhsT=hq[i][0][:].bitcast(FP8X4), lhsT_scale=hq[i][1][:],
+                rhs=bq[c][0][:].bitcast(FP8X4), rhs_scale=bq[c][1][:],
+                start=False, stop=True,
+            )
+            y_bank[unit] = acc
+
+        def add_bias(unit):
+            i, c = unit
+            t = staged("yf", [P, PASS], F32, 14)
+            nc.vector.tensor_tensor(out=t[:], in0=res_sb[unit], in1=bias_bc[:, c * PASS:(c + 1) * PASS], op=ADD)
+            y_f32[unit] = t
+
+        def finish_y(unit):
+            i, c = unit
+            acc = y_bank[unit]
+            t = y_f32[unit]
+            nc.vector.tensor_tensor(out=t[:], in0=acc[:], in1=t[:], op=ADD)
+            nc.sync.dma_start(out=out_0[i * P:(i + 1) * P, c * PASS:(c + 1) * PASS], in_=t[:])
+
+        def round_y(unit):
+            t = staged("ybf", [P, PASS], BF16, 6)
+            nc.scalar.copy(out=sorted_out(t[:]), in_=sorted_in(y_f32[unit][:]))
+            y_bf[unit] = t
+
+        def copy_y(src, slot):
+            grouped = staged("yg", [P, PASS], BF16, 4)
+            copy_pair(grouped[:].bitcast(F32), src, slot)
+            return grouped
+
+        def quantize_y(unit, grouped):
+            i, c = unit
+            codes, first, last = words[unit]
+            cols = slice((i - first) * P, (i - first + 1) * P)
+            quantize(codes[:, cols], planes[i][:, c, cols], grouped[:])
+            if i == last - 1:
+                dst = out_1[c].rearrange("p m t -> p (m t)").bitcast(I32)[:, first * P:last * P]
+                nc.sync.dma_start(out=dst, in_=codes[:].bitcast(I32))
+                if c == GROUPS - 1:
+                    queue = nc.scalar if last == TILES else nc.sync
+                    rows = out_2.bitcast(I32)[:, :, first * P // 4:last * P // 4]
+                    for q in range(4):
+                        queue.dma_start(
+                            out=rows[:, 4 * q:4 * q + 4, :].rearrange("g r m -> r g m"),
+                            in_=planes[i][:].bitcast(I32)[32 * q:32 * q + 4, :, :],
+                        )
+
+        def finish_h(i, src, slot):
+            grouped = staged("hg", [P, R], BF16, 2)
+            copy_pair(grouped[:].bitcast(F32), src, slot)
+            codes = kept("hq%d" % i, [P, P], U32)
+            scales = kept("hsc%d" % i, [P, P], U8)
+            quantize(codes[:], scales[:], grouped[:])
+            hq[i] = (codes, scales)
+
+        def transpose_pairs(sources):
+            places = []
+            for n in range(len(sources)):
+                if n % 2 == 0:
+                    t = bank("t", [P, 4, P])
+                transpose_pair(t, 2 * (n % 2), word_halves(sources[n]))
+                places.append((t, 2 * (n % 2)))
+            return places
+
+        def finish_planes(done, places, between):
+            grouped = [copy_y(*place) for place in places]
+            round_y(between)
+            for n in range(len(done)):
+                quantize_y(done[n], grouped[n])
+
+        banks = transpose_x(0)
+        finish_x(0, 0, banks)
+        finish_x(0, 1, banks)
+        bias_words = bias_col[:].bitcast(F32)
+        bias_banks = [bank("t", [P, 4, P]), bank("t", [P, 4, P])]
+        for c in range(GROUPS):
+            src = [bias_words[:, 2 * c + u:2 * c + u + 1].to_broadcast([P, P]) for u in range(2)]
+            transpose_pair(bias_banks[c // 2], 2 * (c % 2), src)
+        for c in range(GROUPS):
+            copy_pair(bias_bc[:].bitcast(F32)[:, c * 256:(c + 1) * 256], bias_banks[c // 2], 2 * (c % 2))
+        multiply_h(0)
+        banks = transpose_x(1)
+        drop_h(0)
+        finish_x(1, 0, banks)
+        finish_x(1, 1, banks)
+        banks = transpose_x(2)
+        finish_x(2, 0, banks)
+        group_b_vector(0)
+        finish_x(2, 1, banks)
+        group_b_scalar(0, 1)
+        multiply_h(1)
+        multiply_h(2)
+        drop_h(1)
+        places = transpose_pairs([h_bf[0], h_bf[1]])
+        quantize_b(0)
+        add_bias((0, 0))
+        finish_h(0, *places[0])
+        finish_h(1, *places[1])
+        drop_h(2)
+        multiply_y((0, 0))
+        finish_y((0, 0))
+        group_b_scalar(1, 1)
+        round_y((0, 0))
+        add_bias((1, 0))
+        add_bias((2, 0))
+        multiply_y((1, 0))
+        places = transpose_pairs([h_bf[2], y_bf[(0, 0)]])
+        finish_y((1, 0))
+        finish_h(2, *places[0])
+        group_b_vector(1)
+        finish_planes([(0, 0)], places[1:], (1, 0))
+        quantize_b(1)
+        sort_x(HEAD)
+        group_b_scalar(2, 1)
+        add_bias((0, 1))
+        multiply_y((2, 0))
+        finish_y((2, 0))
+        round_y((2, 0))
+        add_bias((1, 1))
+        multiply_y((0, 1))
+        finish_y((0, 1))
+        round_y((0, 1))
+        add_bias((2, 1))
+        multiply_y((1, 1))
+        finish_y((1, 1))
+        round_y((1, 1))
+        group_b_vector(2)
+        multiply_y((2, 1))
+
+        def step(h_tile, x_tile, done, last, todo):
+            places = transpose_pairs([h_bf[h_tile], y_bf[done[0]]]) if h_tile is not None else []
+            banks = transpose_x(x_tile) if x_tile is not None else None
+            places = places + transpose_pairs([y_bf[unit] for unit in done[len(places) // 2:]])
+            finish_y(last)
+            if h_tile is None:
+                quantize_b(GROUPS - 1)
+            if h_tile is not None:
+                finish_h(h_tile, *places[0])
+                places = places[1:]
+            add_bias(todo[0])
+            if x_tile is not None:
+                finish_x(x_tile, 0, banks)
+                finish_x(x_tile, 1, banks)
+            add_bias(todo[1])
+            finish_planes(done, places, last)
+            if x_tile is not None and x_tile + 1 < TILES:
+                sort_x(x_tile + 1)
+            multiply_y(todo[0])
+            finish_y(todo[0])
+            round_y(todo[0])
+            add_bias(todo[2])
+            multiply_y(todo[1])
+            finish_y(todo[1])
+            round_y(todo[1])
+            if x_tile is not None:
+                multiply_h(x_tile)
+                drop_h(x_tile)
+            multiply_y(todo[2])
+
+        step(None, HEAD, [(1, 0), (2, 0), (0, 1), (1, 1)], (2, 1), [(0, 2), (1, 2), (2, 2)])
+        done = [(2, 1), (0, 2), (1, 2)]
+        for i in range(HEAD, TILES):
+            step(i, i + 1 if i + 1 < TILES else None, done, (i - 1, 2), [(i, c) for c in range(GROUPS)])
+            done = [(i - 1, 2), (i, 0), (i, 1)]
+
+        last = (TILES - 1, GROUPS - 1)
+        places = transpose_pairs([y_bf[unit] for unit in done])
+        rounded = staged("ybf", [P, PASS], BF16, 6)
+        nc.vector.tensor_tensor(
+            out=sorted_out(rounded[:]), in0=sorted_in(y_bank[last][:]), in1=sorted_in(y_f32[last][:]), op=ADD
+        )
+        finish_y(last)
+        t = bank("t", [P, 4, P])
+        transpose_pair(t, 0, word_halves(rounded))
+        places.append((t, 0))
+        done.append(last)
+        for n in range(len(done)):
+            quantize_y(done[n], copy_y(*places[n]))

@@ -37,16 +37,16 @@ def tile_lora_dropout_output_projection_h1_kernel(
         ctx.enter_context(tc.manual_schedule())
 
         def kept(name, shape, dtype):
-            return keep.tile(shape, dtype, name=name, align_bytes=64)
+            return keep.tile(shape, dtype, name=name, align_bytes=256 if dtype in (U8, U32) else 64)
 
         def staged(tag, shape, dtype, bufs):
             return stage.tile(shape, dtype, name=tag, tag=tag, bufs=bufs, align_bytes=64)
 
-        turn = {"t": 0, "m": 0}
+        turn = {"bank": 0}
 
-        def bank(kind, shape):
-            tag = "%s%d" % (kind, turn[kind] % 4)
-            turn[kind] = turn[kind] + 1
+        def bank(shape):
+            tag = "bank%d" % (turn["bank"] % 8)
+            turn["bank"] = turn["bank"] + 1
             return psum.tile(shape, F32, name=tag, tag=tag)
 
         ident = kept("ident", [P, P], F32)
@@ -68,19 +68,26 @@ def tile_lora_dropout_output_projection_h1_kernel(
             for r in range(4):
                 nc.sync.dma_start(out=plane[:].bitcast(I32)[r:P:32, :, :], in_=by_r[r])
 
+        def load_x_half(h):
+            t = kept("x0_%d" % h, [P, K // 2], BF16)
+            nc.sync.dma_start(out=t[:], in_=x[0:P, h * (K // 2):(h + 1) * (K // 2)])
+            x_half[(0, h)] = t[:].bitcast(F32)
+
         def load_x(i):
-            rows = x[i * P:(i + 1) * P, :]
-            if i == 0:
-                for h in range(2):
-                    t = kept("x%d_%d" % (i, h), [P, K // 2], BF16)
-                    nc.sync.dma_start(out=t[:], in_=rows[:, h * (K // 2):(h + 1) * (K // 2)])
-                    x_half[(i, h)] = t[:].bitcast(F32)
-            else:
-                t = kept("x%d" % i, [P, K], BF16)
-                nc.sync.dma_start(out=t[:], in_=rows)
-                for h in range(2):
-                    x_half[(i, h)] = t[:].bitcast(F32)[:, h * (K // 4):(h + 1) * (K // 4)]
-                x_half[i] = t[:].bitcast(F32)
+            t = kept("x%d" % i, [P, K], BF16)
+            nc.sync.dma_start(out=t[:], in_=x[i * P:(i + 1) * P, :])
+            for h in range(2):
+                x_half[(i, h)] = t[:].bitcast(F32)[:, h * (K // 4):(h + 1) * (K // 4)]
+            x_half[i] = t[:].bitcast(F32)
+
+        a_sb = {}
+
+        def load_a(h):
+            t = kept("a%d" % h, [P, 2, 2 * R], U8)
+            src = a_words.bitcast(I32)[2 * h:2 * h + 2].rearrange("g p n -> p g n")
+            nc.sync.dma_start(out=t[:].bitcast(I32), in_=src)
+            for g in range(2):
+                a_sb[2 * h + g] = t[:, g, :]
 
         def load_drop(i):
             t = kept("drop%d" % i, [P, R], BF16)
@@ -111,18 +118,19 @@ def tile_lora_dropout_output_projection_h1_kernel(
             for c in range(GROUPS):
                 res_sb[(i, c)] = t[:, c * PASS:(c + 1) * PASS]
 
-        load_x(0)
+        load_x_half(0)
+        load_x_half(1)
         bias_col = kept("bias_col", [P, GROUPS * 4], BF16)
         nc.sync.dma_start(
             out=bias_col[:].rearrange("p (c e) -> p c e", e=4),
             in_=bias.rearrange("(c p e) -> p c e", p=P, e=4),
         )
-        a_sb = kept("a_sb", [P, PASSES, 2 * R], U8)
-        nc.sync.dma_start(out=a_sb[:].bitcast(I32), in_=a_words.bitcast(I32).rearrange("g p n -> p g n"))
         load_scales(a_sc, a_scales.bitcast(I32))
+        load_a(0)
+        load_a(1)
         load_x(1)
-        load_drop(0)
         load_x(2)
+        load_drop(0)
         load_b(0)
         load_drop(1)
         load_w(0)
@@ -132,17 +140,15 @@ def tile_lora_dropout_output_projection_h1_kernel(
         load_b(1)
         load_w(1)
         load_scales(w_sc_rest, w0_scales.bitcast(I32)[:, :, PASS // 4:N // 4])
-        load_res_head(1)
         load_x(3)
+        load_res_head(1)
         load_b(2)
         load_w(2)
         load_drop(3)
         load_res_head(2)
-        for i in range(HEAD + 1, TILES):
-            load_x(i)
-            load_drop(i)
-            load_res(i - 1)
-        load_res(TILES - 1)
+        load_x(HEAD + 1)
+        load_drop(HEAD + 1)
+        load_res(HEAD)
 
         def w_scale(g, c):
             if c == 0:
@@ -202,19 +208,19 @@ def tile_lora_dropout_output_projection_h1_kernel(
             )
             x_sorted[i] = t
 
+        def transpose_x_half(i, h):
+            t = bank([P, 4, P])
+            for g in range(2):
+                if i in x_sorted:
+                    at = (2 * h + g) * 256
+                    src = [x_sorted[i][:, at:at + P], x_sorted[i][:, at + P:at + 2 * P]]
+                else:
+                    src = [x_half[(i, h)][:, g * 256 + u:(g + 1) * 256:2] for u in range(2)]
+                transpose_pair(t, 2 * g, src)
+            return t
+
         def transpose_x(i):
-            banks = []
-            for h in range(2):
-                t = bank("t", [P, 4, P])
-                for g in range(2):
-                    if i in x_sorted:
-                        at = (2 * h + g) * 256
-                        src = [x_sorted[i][:, at:at + P], x_sorted[i][:, at + P:at + 2 * P]]
-                    else:
-                        src = [x_half[(i, h)][:, g * 256 + u:(g + 1) * 256:2] for u in range(2)]
-                    transpose_pair(t, 2 * g, src)
-                banks.append(t)
-            return banks
+            return [transpose_x_half(i, h) for h in range(2)]
 
         def finish_x(i, h, banks):
             grouped = staged("xg", [P, K // 2], BF16, 3)
@@ -253,12 +259,12 @@ def tile_lora_dropout_output_projection_h1_kernel(
             bq[c] = (codes, scales)
 
         def multiply_h(i):
-            acc = bank("m", [P, R])
+            acc = bank([P, R])
             for g in range(PASSES):
                 codes, scales = xq[(i, g)]
                 nc.tensor.matmul_mx(
                     out=acc[:], lhsT=codes.bitcast(FP8X4), lhsT_scale=scales,
-                    rhs=a_sb[:, g, :].bitcast(FP4X4), rhs_scale=a_sc[:, g, :],
+                    rhs=a_sb[g].bitcast(FP4X4), rhs_scale=a_sc[:, g, :],
                     start=(g == 0), stop=(g == PASSES - 1),
                 )
             h_bank[i] = acc
@@ -270,26 +276,30 @@ def tile_lora_dropout_output_projection_h1_kernel(
             )
             h_bf[i] = t
 
-        def multiply_y(unit):
+        def multiply_columns(unit, first, width):
             i, c = unit
-            acc = bank("m", [P, PASS])
+            acc = bank([P, width])
+            cols = slice(first, first + width)
             for g in range(PASSES):
                 codes, scales = xq[(i, g)]
                 nc.tensor.matmul_mx(
                     out=acc[:], lhsT=codes.bitcast(FP8X4), lhsT_scale=scales,
-                    rhs=w_sb[c][:, g, :].bitcast(FP4X4), rhs_scale=w_scale(g, c),
+                    rhs=w_sb[c][:, g, 2 * first:2 * (first + width)].bitcast(FP4X4), rhs_scale=w_scale(g, c)[:, cols],
                     start=(g == 0), stop=False,
                 )
             nc.tensor.matmul_mx(
                 out=acc[:], lhsT=hq[i][0][:].bitcast(FP8X4), lhsT_scale=hq[i][1][:],
-                rhs=bq[c][0][:].bitcast(FP8X4), rhs_scale=bq[c][1][:],
+                rhs=bq[c][0][:, cols].bitcast(FP8X4), rhs_scale=bq[c][1][:, cols],
                 start=False, stop=True,
             )
-            y_bank[unit] = acc
+            return acc
+
+        def multiply_y(unit):
+            y_bank[unit] = multiply_columns(unit, 0, PASS)
 
         def add_bias(unit):
             i, c = unit
-            t = staged("yf", [P, PASS], F32, 14)
+            t = staged("yf", [P, PASS], F32, 11)
             nc.vector.tensor_tensor(out=t[:], in0=res_sb[unit], in1=bias_bc[:, c * PASS:(c + 1) * PASS], op=ADD)
             y_f32[unit] = t
 
@@ -301,7 +311,7 @@ def tile_lora_dropout_output_projection_h1_kernel(
             nc.sync.dma_start(out=out_0[i * P:(i + 1) * P, c * PASS:(c + 1) * PASS], in_=t[:])
 
         def round_y(unit):
-            t = staged("ybf", [P, PASS], BF16, 6)
+            t = staged("ybf", [P, PASS], BF16, 7)
             nc.scalar.copy(out=sorted_out(t[:]), in_=sorted_in(y_f32[unit][:]))
             y_bf[unit] = t
 
@@ -339,7 +349,7 @@ def tile_lora_dropout_output_projection_h1_kernel(
             places = []
             for n in range(len(sources)):
                 if n % 2 == 0:
-                    t = bank("t", [P, 4, P])
+                    t = bank([P, 4, P])
                 transpose_pair(t, 2 * (n % 2), word_halves(sources[n]))
                 places.append((t, 2 * (n % 2)))
             return places
@@ -354,107 +364,118 @@ def tile_lora_dropout_output_projection_h1_kernel(
         finish_x(0, 0, banks)
         finish_x(0, 1, banks)
         bias_words = bias_col[:].bitcast(F32)
-        bias_banks = [bank("t", [P, 4, P]), bank("t", [P, 4, P])]
+        bias_banks = [bank([P, 4, P]), bank([P, 4, P])]
         for c in range(GROUPS):
             src = [bias_words[:, 2 * c + u:2 * c + u + 1].to_broadcast([P, P]) for u in range(2)]
             transpose_pair(bias_banks[c // 2], 2 * (c % 2), src)
         for c in range(GROUPS):
             copy_pair(bias_bc[:].bitcast(F32)[:, c * 256:(c + 1) * 256], bias_banks[c // 2], 2 * (c % 2))
         multiply_h(0)
-        banks = transpose_x(1)
+        banks1 = transpose_x(1)
         drop_h(0)
-        finish_x(1, 0, banks)
-        finish_x(1, 1, banks)
-        banks = transpose_x(2)
-        finish_x(2, 0, banks)
+        banks2 = transpose_x(2)
+        places = transpose_pairs([h_bf[0]])
+        finish_x(1, 0, banks1)
+        finish_x(1, 1, banks1)
+        finish_x(2, 0, banks2)
         group_b_vector(0)
-        finish_x(2, 1, banks)
+        finish_x(2, 1, banks2)
+        finish_h(0, *places[0])
         group_b_scalar(0, 1)
         multiply_h(1)
         multiply_h(2)
         drop_h(1)
-        places = transpose_pairs([h_bf[0], h_bf[1]])
         quantize_b(0)
-        add_bias((0, 0))
-        finish_h(0, *places[0])
-        finish_h(1, *places[1])
         drop_h(2)
+        add_bias((0, 0))
+        add_bias((1, 0))
         multiply_y((0, 0))
+        places = transpose_pairs([h_bf[1], h_bf[2]])
         finish_y((0, 0))
+        finish_h(1, *places[0])
+        finish_h(2, *places[1])
         group_b_scalar(1, 1)
         round_y((0, 0))
-        add_bias((1, 0))
-        add_bias((2, 0))
-        multiply_y((1, 0))
-        places = transpose_pairs([h_bf[2], y_bf[(0, 0)]])
-        finish_y((1, 0))
-        finish_h(2, *places[0])
         group_b_vector(1)
-        finish_planes([(0, 0)], places[1:], (1, 0))
+        multiply_y((1, 0))
+        finish_y((1, 0))
+        round_y((1, 0))
         quantize_b(1)
-        sort_x(HEAD)
-        group_b_scalar(2, 1)
-        add_bias((0, 1))
+        add_bias((2, 0))
         multiply_y((2, 0))
+        sort_x(HEAD)
         finish_y((2, 0))
         round_y((2, 0))
-        add_bias((1, 1))
+        add_bias((0, 1))
         multiply_y((0, 1))
         finish_y((0, 1))
         round_y((0, 1))
-        add_bias((2, 1))
+        add_bias((1, 1))
         multiply_y((1, 1))
-        finish_y((1, 1))
-        round_y((1, 1))
-        group_b_vector(2)
-        multiply_y((2, 1))
 
-        def step(h_tile, x_tile, done, last, todo):
-            places = transpose_pairs([h_bf[h_tile], y_bf[done[0]]]) if h_tile is not None else []
+        final = (TILES - 1, GROUPS - 1)
+
+        def step(h_tile, x_tile, done, last, todo, b_group):
+            lead = 1 if h_tile is not None else 0
+            if x_tile is not None and x_tile + 2 < TILES:
+                load_x(x_tile + 2)
+                load_drop(x_tile + 2)
+            if x_tile is not None and x_tile + 1 < TILES:
+                load_res(x_tile + 1)
+            places = transpose_pairs([h_bf[h_tile], y_bf[done[0]]]) if lead else []
             banks = transpose_x(x_tile) if x_tile is not None else None
-            places = places + transpose_pairs([y_bf[unit] for unit in done[len(places) // 2:]])
+            places = places + transpose_pairs([y_bf[unit] for unit in done[lead:]])
             finish_y(last)
-            if h_tile is None:
-                quantize_b(GROUPS - 1)
-            if h_tile is not None:
+            if lead:
                 finish_h(h_tile, *places[0])
-                places = places[1:]
-            add_bias(todo[0])
+            if b_group is not None:
+                group_b_scalar(b_group, 1)
+                group_b_vector(b_group)
+            add_bias(todo[1])
+            if b_group is not None:
+                quantize_b(b_group)
             if x_tile is not None:
                 finish_x(x_tile, 0, banks)
+            if x_tile is not None:
                 finish_x(x_tile, 1, banks)
-            add_bias(todo[1])
-            finish_planes(done, places, last)
+            add_bias(todo[2])
+            finish_planes(done, places[lead:], last)
             if x_tile is not None and x_tile + 1 < TILES:
                 sort_x(x_tile + 1)
-            multiply_y(todo[0])
-            finish_y(todo[0])
-            round_y(todo[0])
-            add_bias(todo[2])
-            multiply_y(todo[1])
-            finish_y(todo[1])
-            round_y(todo[1])
-            if x_tile is not None:
-                multiply_h(x_tile)
-                drop_h(x_tile)
-            multiply_y(todo[2])
+            for n in range(len(todo) - 1):
+                multiply_y(todo[n])
+                finish_y(todo[n])
+                round_y(todo[n])
+                if n + 3 < len(todo):
+                    add_bias(todo[n + 3])
+                if n == 1 and x_tile is not None:
+                    multiply_h(x_tile)
+                    drop_h(x_tile)
+            if todo[-1] != final:
+                multiply_y(todo[-1])
+                add_bias((x_tile, 0))
 
-        step(None, HEAD, [(1, 0), (2, 0), (0, 1), (1, 1)], (2, 1), [(0, 2), (1, 2), (2, 2)])
-        done = [(2, 1), (0, 2), (1, 2)]
+        add_bias((2, 1))
+        step(None, HEAD, [(0, 0), (1, 0), (2, 0), (0, 1)], (1, 1), [(2, 1), (0, 2), (1, 2), (2, 2)], 2)
+        done = [(1, 1), (2, 1), (0, 2), (1, 2)]
         for i in range(HEAD, TILES):
-            step(i, i + 1 if i + 1 < TILES else None, done, (i - 1, 2), [(i, c) for c in range(GROUPS)])
+            step(i, i + 1 if i + 1 < TILES else None, done, (i - 1, 2), [(i, c) for c in range(GROUPS)], None)
             done = [(i - 1, 2), (i, 0), (i, 1)]
 
-        last = (TILES - 1, GROUPS - 1)
+        result = kept("y_final", [P, PASS], F32)
+        rounded = staged("ybf", [P, PASS], BF16, 7)
+        for j in range(4):
+            acc = multiply_columns(final, j * P, P)
+            part = y_f32[final][:, j * P:(j + 1) * P]
+            nc.vector.tensor_tensor(
+                out=sorted_out(rounded[:])[:, :, j * 32:(j + 1) * 32, :], in0=sorted_in(acc[:]), in1=sorted_in(part), op=ADD
+            )
+            nc.vector.tensor_tensor(out=result[:, j * P:(j + 1) * P], in0=acc[:], in1=part, op=ADD)
+        nc.sync.dma_start(out=out_0[M - P:M, N - PASS:N], in_=result[:])
         places = transpose_pairs([y_bf[unit] for unit in done])
-        rounded = staged("ybf", [P, PASS], BF16, 6)
-        nc.vector.tensor_tensor(
-            out=sorted_out(rounded[:]), in0=sorted_in(y_bank[last][:]), in1=sorted_in(y_f32[last][:]), op=ADD
-        )
-        finish_y(last)
-        t = bank("t", [P, 4, P])
+        t = bank([P, 4, P])
         transpose_pair(t, 0, word_halves(rounded))
         places.append((t, 0))
-        done.append(last)
+        done.append(final)
         for n in range(len(done)):
             quantize_y(done[n], copy_y(*places[n]))

@@ -19,11 +19,22 @@ ADD = mybir.AluOpType.add
 
 P = 128
 PASS = 512
+PAIRS = PASS // 2
 PASSES = K // PASS
 TILES = M // P
 GROUPS = N // PASS
+BANKS = 8
+HALVES = ([0, 1], [2, 3])
 HEAD = 3
-BLOCKS = [(0, 3), (3, 6), (6, 8)]
+STORE_BLOCKS = [(0, 3), (3, 6), (6, 8)]
+X_SORTED_BUFS = 2
+X_GROUPED_BUFS = 3
+B_GROUPED_BUFS = 2
+H_ROUNDED_BUFS = 3
+H_GROUPED_BUFS = 2
+Y_BUFS = 11
+Y_ROUNDED_BUFS = 7
+Y_GROUPED_BUFS = 5
 
 
 def tile_lora_dropout_output_projection_h1_kernel(
@@ -42,52 +53,55 @@ def tile_lora_dropout_output_projection_h1_kernel(
         def staged(tag, shape, dtype, bufs):
             return stage.tile(shape, dtype, name=tag, tag=tag, bufs=bufs, align_bytes=64)
 
-        turn = {"bank": 0}
+        banks_taken = []
 
         def bank(shape):
-            tag = "bank%d" % (turn["bank"] % 8)
-            turn["bank"] = turn["bank"] + 1
+            tag = "bank%d" % (len(banks_taken) % BANKS)
+            banks_taken.append(tag)
             return psum.tile(shape, F32, name=tag, tag=tag)
 
         ident = kept("ident", [P, P], F32)
         make_identity(nc, ident[:])
-        a_sc = kept("a_sc", [P, PASSES, R], U8)
-        w_sc_first = kept("w_sc_first", [P, PASSES, PASS], U8)
-        w_sc_rest = kept("w_sc_rest", [P, PASSES, N - PASS], U8)
-        for plane in (a_sc, w_sc_first, w_sc_rest):
+
+        a_plane = kept("a_plane", [P, PASSES, R], U8)
+        w_plane_first = kept("w_plane_first", [P, PASSES, PASS], U8)
+        w_plane_rest = kept("w_plane_rest", [P, PASSES, N - PASS], U8)
+        for plane in (a_plane, w_plane_first, w_plane_rest):
             nc.vector.memset(plane[:].bitcast(I32), 0)
 
-        x_half = {}
-        drop_sb = {}
-        res_sb = {}
+        x_tile_pairs = {}
+        x_pass_pairs = {}
+        a_sb = {}
         w_sb = {}
         b_sb = {}
+        drop_sb = {}
+        res_sb = {}
 
         def load_scales(plane, rows):
             by_r = rows.rearrange("g (q r) n -> r q g n", r=4)
             for r in range(4):
                 nc.sync.dma_start(out=plane[:].bitcast(I32)[r:P:32, :, :], in_=by_r[r])
 
-        def load_x_half(h):
-            t = kept("x0_%d" % h, [P, K // 2], BF16)
-            nc.sync.dma_start(out=t[:], in_=x[0:P, h * (K // 2):(h + 1) * (K // 2)])
-            x_half[(0, h)] = t[:].bitcast(F32)
+        def load_x_first():
+            for first, end in ((0, 1), (1, 2), (2, 4)):
+                t = kept("x0_%d" % first, [P, (end - first) * PASS], BF16)
+                nc.sync.dma_start(out=t[:], in_=x[0:P, first * PASS:end * PASS])
+                for g in range(first, end):
+                    x_pass_pairs[(0, g)] = t[:].bitcast(F32)[:, (g - first) * PAIRS:(g - first + 1) * PAIRS]
 
         def load_x(i):
             t = kept("x%d" % i, [P, K], BF16)
             nc.sync.dma_start(out=t[:], in_=x[i * P:(i + 1) * P, :])
-            for h in range(2):
-                x_half[(i, h)] = t[:].bitcast(F32)[:, h * (K // 4):(h + 1) * (K // 4)]
-            x_half[i] = t[:].bitcast(F32)
+            x_tile_pairs[i] = t[:].bitcast(F32)
+            for g in range(PASSES):
+                x_pass_pairs[(i, g)] = x_tile_pairs[i][:, g * PAIRS:(g + 1) * PAIRS]
 
-        a_sb = {}
-
-        def load_a(h):
-            t = kept("a%d" % h, [P, 2, 2 * R], U8)
-            src = a_words.bitcast(I32)[2 * h:2 * h + 2].rearrange("g p n -> p g n")
+        def load_a(half):
+            t = kept("a%d" % half, [P, 2, 2 * R], U8)
+            src = a_words.bitcast(I32)[2 * half:2 * half + 2].rearrange("g p n -> p g n")
             nc.sync.dma_start(out=t[:].bitcast(I32), in_=src)
-            for g in range(2):
-                a_sb[2 * h + g] = t[:, g, :]
+            for n in range(2):
+                a_sb[2 * half + n] = t[:, n, :]
 
         def load_drop(i):
             t = kept("drop%d" % i, [P, R], BF16)
@@ -96,17 +110,18 @@ def tile_lora_dropout_output_projection_h1_kernel(
 
         def load_w(c):
             t = kept("w%d" % c, [P, PASSES, 2 * PASS], U8)
-            src = w0_words.bitcast(I32)[:, :, c * 256:(c + 1) * 256].rearrange("g p n -> p g n")
+            per_group = 2 * PASS // 4
+            src = w0_words.bitcast(I32)[:, :, c * per_group:(c + 1) * per_group].rearrange("g p n -> p g n")
             nc.sync.dma_start(out=t[:].bitcast(I32), in_=src)
             w_sb[c] = t
 
         def load_b(c):
             t = kept("b%d" % c, [P, 4, PASS], BF16)
-            nc.sync.dma_start(out=t[:], in_=b[:, c * PASS:(c + 1) * PASS].rearrange("(p j) n -> p j n", j=4))
+            nc.sync.dma_start(out=t[:], in_=b[:, c * PASS:(c + 1) * PASS].rearrange("(p t) n -> p t n", t=4))
             b_sb[c] = t
 
         def load_res_head(c):
-            t = kept("resh%d" % c, [P, HEAD, PASS], BF16)
+            t = kept("res_head%d" % c, [P, HEAD, PASS], BF16)
             src = residual[0:HEAD * P, c * PASS:(c + 1) * PASS].rearrange("(i p) n -> p i n", p=P)
             nc.sync.dma_start(out=t[:], in_=src)
             for i in range(HEAD):
@@ -118,14 +133,13 @@ def tile_lora_dropout_output_projection_h1_kernel(
             for c in range(GROUPS):
                 res_sb[(i, c)] = t[:, c * PASS:(c + 1) * PASS]
 
-        load_x_half(0)
-        load_x_half(1)
+        load_x_first()
         bias_col = kept("bias_col", [P, GROUPS * 4], BF16)
         nc.sync.dma_start(
-            out=bias_col[:].rearrange("p (c e) -> p c e", e=4),
-            in_=bias.rearrange("(c p e) -> p c e", p=P, e=4),
+            out=bias_col[:].rearrange("p (c t) -> p c t", t=4),
+            in_=bias.rearrange("(c p t) -> p c t", p=P, t=4),
         )
-        load_scales(a_sc, a_scales.bitcast(I32))
+        load_scales(a_plane, a_scales.bitcast(I32))
         load_a(0)
         load_a(1)
         load_x(1)
@@ -134,162 +148,174 @@ def tile_lora_dropout_output_projection_h1_kernel(
         load_b(0)
         load_drop(1)
         load_w(0)
-        load_scales(w_sc_first, w0_scales.bitcast(I32)[:, :, 0:PASS // 4])
+        load_scales(w_plane_first, w0_scales.bitcast(I32)[:, :, 0:PASS // 4])
         load_drop(2)
         load_res_head(0)
         load_b(1)
         load_w(1)
-        load_scales(w_sc_rest, w0_scales.bitcast(I32)[:, :, PASS // 4:N // 4])
-        load_x(3)
+        load_scales(w_plane_rest, w0_scales.bitcast(I32)[:, :, PASS // 4:N // 4])
+        load_x(HEAD)
         load_res_head(1)
         load_b(2)
         load_w(2)
-        load_drop(3)
+        load_drop(HEAD)
         load_res_head(2)
         load_x(HEAD + 1)
         load_drop(HEAD + 1)
         load_res(HEAD)
 
-        def w_scale(g, c):
+        def w_plane(g, c):
             if c == 0:
-                return w_sc_first[:, g, :]
-            return w_sc_rest[:, g, (c - 1) * PASS:c * PASS]
+                return w_plane_first[:, g, :]
+            return w_plane_rest[:, g, (c - 1) * PASS:c * PASS]
 
-        bias_bc = kept("bias_bc", [P, N], BF16)
-        xq = {}
-        hq = {}
-        bq = {}
+        bias_rows = kept("bias_rows", [P, N], BF16)
         x_sorted = {}
+        x_q = {}
         h_bank = {}
-        h_bf = {}
-        y_f32 = {}
+        h_rounded = {}
+        h_q = {}
+        b_grouped = {}
+        b_q = {}
         y_bank = {}
-        y_bf = {}
-        words = {}
-        planes = {}
-        for first, last in BLOCKS:
-            width = (last - first) * P
-            plane = kept("ysc%d" % first, [P, GROUPS, width], U8)
+        y_f32 = {}
+        y_rounded = {}
+        y_words = {}
+        y_plane = {}
+        for first, end in STORE_BLOCKS:
+            width = (end - first) * P
+            plane = kept("y_plane%d" % first, [P, GROUPS, width], U8)
             for c in range(GROUPS):
-                codes = kept("yq%d_%d" % (first, c), [P, width], U32)
-                for i in range(first, last):
-                    words[(i, c)] = (codes, first, last)
-            for i in range(first, last):
-                planes[i] = plane
+                words = kept("y_words%d_%d" % (first, c), [P, width], U32)
+                for i in range(first, end):
+                    y_words[(i, c)] = (words, first, end)
+            for i in range(first, end):
+                y_plane[i] = plane
 
-        def sorted_out(ap):
+        def as_sorted(ap):
             return ap.rearrange("p (u q e) -> p u q e", u=2, e=2)
 
-        def sorted_in(ap):
+        def as_natural(ap):
             return ap.rearrange("p (q u e) -> p u q e", u=2, e=2)
 
-        def transpose_pair(dst, slot, sources):
+        def transpose_even_odd(dst, slot, even_odd):
             for u in range(2):
-                nc.tensor.transpose(dst[:, slot + u, :], sources[u], ident[:])
+                nc.tensor.transpose(dst[:, slot + u, :], even_odd[u], ident[:])
 
-        def word_halves(tile_bf):
-            w = tile_bf[:].bitcast(F32)
-            return [w[:, 0:P], w[:, P:2 * P]]
+        def transpose_sorted(sources):
+            places = []
+            for n in range(len(sources)):
+                if n % 2 == 0:
+                    t = bank([P, 4, P])
+                pairs = sources[n][:].bitcast(F32)
+                transpose_even_odd(t, 2 * (n % 2), [pairs[:, 0:P], pairs[:, P:2 * P]])
+                places.append((t, 2 * (n % 2)))
+            return places
 
-        def copy_pair(dst_words, src, slot):
-            nc.scalar.copy(
-                out=dst_words.rearrange("p (r u) -> p r u", u=2),
-                in_=src[:, slot:slot + 2, :].rearrange("p u r -> p r u"),
+        def copy_side_by_side(dst_pairs, src, slot, copy):
+            copy(
+                out=dst_pairs.rearrange("p (m u) -> p m u", u=2),
+                in_=src[:, slot:slot + 2, :].rearrange("p u m -> p m u"),
             )
 
-        def quantize(codes, scales, grouped):
-            nc.vector.quantize_mx(out=codes.bitcast(FP8X4), scales=scales, in_=grouped)
+        def quantize(words, plane, grouped):
+            nc.vector.quantize_mx(out=words.bitcast(FP8X4), scales=plane, in_=grouped)
 
         def sort_x(i):
-            t = staged("xs", [P, K // 2], F32, 2)
+            t = staged("x_sorted", [P, K // 2], F32, X_SORTED_BUFS)
             nc.scalar.copy(
                 out=t[:].rearrange("p (g u q) -> p g u q", u=2, q=P),
-                in_=x_half[i].rearrange("p (g q u) -> p g u q", u=2, q=P),
+                in_=x_tile_pairs[i].rearrange("p (g q u) -> p g u q", u=2, q=P),
             )
             x_sorted[i] = t
 
-        def transpose_x_half(i, h):
-            t = bank([P, 4, P])
-            for g in range(2):
+        def transpose_x(i, passes):
+            t = bank([P, 2 * len(passes), P])
+            for n in range(len(passes)):
+                g = passes[n]
                 if i in x_sorted:
-                    at = (2 * h + g) * 256
-                    src = [x_sorted[i][:, at:at + P], x_sorted[i][:, at + P:at + 2 * P]]
+                    even_odd = [x_sorted[i][:, (2 * g + u) * P:(2 * g + u + 1) * P] for u in range(2)]
                 else:
-                    src = [x_half[(i, h)][:, g * 256 + u:(g + 1) * 256:2] for u in range(2)]
-                transpose_pair(t, 2 * g, src)
-            return t
+                    even_odd = [x_pass_pairs[(i, g)][:, u:PAIRS:2] for u in range(2)]
+                transpose_even_odd(t, 2 * n, even_odd)
+            return (i, passes, t)
 
-        def transpose_x(i):
-            return [transpose_x_half(i, h) for h in range(2)]
-
-        def finish_x(i, h, banks):
-            grouped = staged("xg", [P, K // 2], BF16, 3)
+        def quantize_x(piece):
+            i, passes, t = piece
+            count = len(passes)
+            grouped = staged("x_grouped", [P, count * PASS], BF16, X_GROUPED_BUFS)
             nc.scalar.copy(
-                out=grouped[:].bitcast(F32).rearrange("p (g r u) -> p g r u", g=2, u=2),
-                in_=banks[h][:].rearrange("p (g u) r -> p g r u", u=2),
+                out=grouped[:].bitcast(F32).rearrange("p (g m u) -> p g m u", g=count, u=2),
+                in_=t[:].rearrange("p (g u) m -> p g m u", u=2),
             )
-            codes = kept("xq%d_%d" % (i, h), [P, 2 * P], U32)
-            scales = kept("xsc%d_%d" % (i, h), [P, 2 * P], U8)
-            quantize(codes[:], scales[:], grouped[:])
-            for g in range(2):
-                xq[(i, 2 * h + g)] = (codes[:, g * P:(g + 1) * P], scales[:, g * P:(g + 1) * P])
+            words = kept("x_words%d_%d" % (i, passes[0]), [P, count * P], U32)
+            plane = kept("x_plane%d_%d" % (i, passes[0]), [P, count * P], U8)
+            quantize(words[:], plane[:], grouped[:])
+            for n in range(count):
+                x_q[(i, passes[n])] = (words[:, n * P:(n + 1) * P], plane[:, n * P:(n + 1) * P])
 
-        b_grouped = {}
-
-        def b_views(c, h):
+        def b_views(c, half):
             if c not in b_grouped:
-                b_grouped[c] = staged("bg", [P, 4 * PASS], BF16, 2)
-            dst = b_grouped[c][:, h * 2 * PASS:(h + 1) * 2 * PASS].rearrange("p (n i t) -> p n t i", i=4, t=4)
-            src = b_sb[c][:, :, h * 256:(h + 1) * 256].rearrange("p t (n i) -> p n t i", i=4)
+                b_grouped[c] = staged("b_grouped", [P, 4 * PASS], BF16, B_GROUPED_BUFS)
+            cols = PASS // 2
+            dst = b_grouped[c][:, half * 4 * cols:(half + 1) * 4 * cols].rearrange("p (n j t) -> p n t j", j=4, t=4)
+            src = b_sb[c][:, :, half * cols:(half + 1) * cols].rearrange("p t (n j) -> p n t j", j=4)
             return dst, src
 
         def group_b_vector(c):
             dst, src = b_views(c, 0)
             nc.vector.tensor_scalar(out=dst, in0=src, scalar1=LORA_SCALE, scalar2=None, op0=MULT)
 
-        def group_b_scalar(c, h):
-            dst, src = b_views(c, h)
+        def group_b_scalar(c):
+            dst, src = b_views(c, 1)
             nc.scalar.activation(out=dst, in_=src, func=mybir.ActivationFunctionType.Copy, scale=LORA_SCALE)
 
         def quantize_b(c):
-            grouped = b_grouped[c]
-            codes = kept("bq%d" % c, [P, PASS], U32)
-            scales = kept("bsc%d" % c, [P, PASS], U8)
-            quantize(codes[:], scales[:], grouped[:])
-            bq[c] = (codes, scales)
+            words = kept("b_words%d" % c, [P, PASS], U32)
+            plane = kept("b_plane%d" % c, [P, PASS], U8)
+            quantize(words[:], plane[:], b_grouped[c][:])
+            b_q[c] = (words, plane)
 
         def multiply_h(i):
             acc = bank([P, R])
             for g in range(PASSES):
-                codes, scales = xq[(i, g)]
+                words, plane = x_q[(i, g)]
                 nc.tensor.matmul_mx(
-                    out=acc[:], lhsT=codes.bitcast(FP8X4), lhsT_scale=scales,
-                    rhs=a_sb[g].bitcast(FP4X4), rhs_scale=a_sc[:, g, :],
+                    out=acc[:], lhsT=words.bitcast(FP8X4), lhsT_scale=plane,
+                    rhs=a_sb[g].bitcast(FP4X4), rhs_scale=a_plane[:, g, :],
                     start=(g == 0), stop=(g == PASSES - 1),
                 )
             h_bank[i] = acc
 
         def drop_h(i):
-            t = staged("hbf", [P, R], BF16, 3)
+            t = staged("h_rounded", [P, R], BF16, H_ROUNDED_BUFS)
             nc.vector.tensor_tensor(
-                out=sorted_out(t[:]), in0=sorted_in(h_bank[i][:]), in1=sorted_in(drop_sb[i][:]), op=MULT
+                out=as_sorted(t[:]), in0=as_natural(h_bank[i][:]), in1=as_natural(drop_sb[i][:]), op=MULT
             )
-            h_bf[i] = t
+            h_rounded[i] = t
+
+        def quantize_h(i, place):
+            grouped = staged("h_grouped", [P, R], BF16, H_GROUPED_BUFS)
+            copy_side_by_side(grouped[:].bitcast(F32), place[0], place[1], nc.scalar.copy)
+            words = kept("h_words%d" % i, [P, P], U32)
+            plane = kept("h_plane%d" % i, [P, P], U8)
+            quantize(words[:], plane[:], grouped[:])
+            h_q[i] = (words, plane)
 
         def multiply_columns(unit, first, width):
             i, c = unit
             acc = bank([P, width])
             cols = slice(first, first + width)
             for g in range(PASSES):
-                codes, scales = xq[(i, g)]
+                words, plane = x_q[(i, g)]
                 nc.tensor.matmul_mx(
-                    out=acc[:], lhsT=codes.bitcast(FP8X4), lhsT_scale=scales,
-                    rhs=w_sb[c][:, g, 2 * first:2 * (first + width)].bitcast(FP4X4), rhs_scale=w_scale(g, c)[:, cols],
+                    out=acc[:], lhsT=words.bitcast(FP8X4), lhsT_scale=plane,
+                    rhs=w_sb[c][:, g, 2 * first:2 * (first + width)].bitcast(FP4X4), rhs_scale=w_plane(g, c)[:, cols],
                     start=(g == 0), stop=False,
                 )
             nc.tensor.matmul_mx(
-                out=acc[:], lhsT=hq[i][0][:].bitcast(FP8X4), lhsT_scale=hq[i][1][:],
-                rhs=bq[c][0][:, cols].bitcast(FP8X4), rhs_scale=bq[c][1][:, cols],
+                out=acc[:], lhsT=h_q[i][0][:].bitcast(FP8X4), lhsT_scale=h_q[i][1][:],
+                rhs=b_q[c][0][:, cols].bitcast(FP8X4), rhs_scale=b_q[c][1][:, cols],
                 start=False, stop=True,
             )
             return acc
@@ -298,90 +324,68 @@ def tile_lora_dropout_output_projection_h1_kernel(
             y_bank[unit] = multiply_columns(unit, 0, PASS)
 
         def add_bias(unit):
-            i, c = unit
-            t = staged("yf", [P, PASS], F32, 11)
-            nc.vector.tensor_tensor(out=t[:], in0=res_sb[unit], in1=bias_bc[:, c * PASS:(c + 1) * PASS], op=ADD)
+            c = unit[1]
+            t = staged("y_f32", [P, PASS], F32, Y_BUFS)
+            nc.vector.tensor_tensor(out=t[:], in0=res_sb[unit], in1=bias_rows[:, c * PASS:(c + 1) * PASS], op=ADD)
             y_f32[unit] = t
 
         def finish_y(unit):
             i, c = unit
-            acc = y_bank[unit]
             t = y_f32[unit]
-            nc.vector.tensor_tensor(out=t[:], in0=acc[:], in1=t[:], op=ADD)
+            nc.vector.tensor_tensor(out=t[:], in0=y_bank[unit][:], in1=t[:], op=ADD)
             nc.sync.dma_start(out=out_0[i * P:(i + 1) * P, c * PASS:(c + 1) * PASS], in_=t[:])
 
         def round_y(unit):
-            t = staged("ybf", [P, PASS], BF16, 7)
-            nc.scalar.copy(out=sorted_out(t[:]), in_=sorted_in(y_f32[unit][:]))
-            y_bf[unit] = t
+            t = staged("y_rounded", [P, PASS], BF16, Y_ROUNDED_BUFS)
+            nc.scalar.copy(out=as_sorted(t[:]), in_=as_natural(y_f32[unit][:]))
+            y_rounded[unit] = t
 
-        def copy_y(src, slot):
-            grouped = staged("yg", [P, PASS], BF16, 4)
-            copy_pair(grouped[:].bitcast(F32), src, slot)
+        def copy_y(place, copy):
+            grouped = staged("y_grouped", [P, PASS], BF16, Y_GROUPED_BUFS)
+            copy_side_by_side(grouped[:].bitcast(F32), place[0], place[1], copy)
             return grouped
 
         def quantize_y(unit, grouped):
             i, c = unit
-            codes, first, last = words[unit]
+            words, first, end = y_words[unit]
             cols = slice((i - first) * P, (i - first + 1) * P)
-            quantize(codes[:, cols], planes[i][:, c, cols], grouped[:])
-            if i == last - 1:
-                dst = out_1[c].rearrange("p m t -> p (m t)").bitcast(I32)[:, first * P:last * P]
-                nc.sync.dma_start(out=dst, in_=codes[:].bitcast(I32))
+            quantize(words[:, cols], y_plane[i][:, c, cols], grouped[:])
+            if i == end - 1:
+                dst = out_1[c].rearrange("p m t -> p (m t)").bitcast(I32)[:, first * P:end * P]
+                nc.sync.dma_start(out=dst, in_=words[:].bitcast(I32))
                 if c == GROUPS - 1:
-                    queue = nc.scalar if last == TILES else nc.sync
-                    rows = out_2.bitcast(I32)[:, :, first * P // 4:last * P // 4]
+                    queue = nc.scalar if end == TILES else nc.sync
+                    rows = out_2.bitcast(I32)[:, :, first * P // 4:end * P // 4]
                     for q in range(4):
                         queue.dma_start(
                             out=rows[:, 4 * q:4 * q + 4, :].rearrange("g r m -> r g m"),
-                            in_=planes[i][:].bitcast(I32)[32 * q:32 * q + 4, :, :],
+                            in_=y_plane[i][:].bitcast(I32)[32 * q:32 * q + 4, :, :],
                         )
 
-        def finish_h(i, src, slot):
-            grouped = staged("hg", [P, R], BF16, 2)
-            copy_pair(grouped[:].bitcast(F32), src, slot)
-            codes = kept("hq%d" % i, [P, P], U32)
-            scales = kept("hsc%d" % i, [P, P], U8)
-            quantize(codes[:], scales[:], grouped[:])
-            hq[i] = (codes, scales)
-
-        def transpose_pairs(sources):
-            places = []
-            for n in range(len(sources)):
-                if n % 2 == 0:
-                    t = bank([P, 4, P])
-                transpose_pair(t, 2 * (n % 2), word_halves(sources[n]))
-                places.append((t, 2 * (n % 2)))
-            return places
-
-        def finish_planes(done, places, between):
-            grouped = [copy_y(*place) for place in places]
-            round_y(between)
-            for n in range(len(done)):
-                quantize_y(done[n], grouped[n])
-
-        banks = transpose_x(0)
-        finish_x(0, 0, banks)
-        finish_x(0, 1, banks)
-        bias_words = bias_col[:].bitcast(F32)
+        pieces = [transpose_x(0, [g]) for g in range(PASSES)]
+        bias_pairs = bias_col[:].bitcast(F32)
         bias_banks = [bank([P, 4, P]), bank([P, 4, P])]
         for c in range(GROUPS):
-            src = [bias_words[:, 2 * c + u:2 * c + u + 1].to_broadcast([P, P]) for u in range(2)]
-            transpose_pair(bias_banks[c // 2], 2 * (c % 2), src)
+            even_odd = [bias_pairs[:, 2 * c + u:2 * c + u + 1].to_broadcast([P, P]) for u in range(2)]
+            transpose_even_odd(bias_banks[c // 2], 2 * (c % 2), even_odd)
+        for piece in pieces:
+            quantize_x(piece)
         for c in range(GROUPS):
-            copy_pair(bias_bc[:].bitcast(F32)[:, c * 256:(c + 1) * 256], bias_banks[c // 2], 2 * (c % 2))
+            dst = bias_rows[:].bitcast(F32)[:, c * PAIRS:(c + 1) * PAIRS]
+            copy_side_by_side(dst, bias_banks[c // 2], 2 * (c % 2), nc.scalar.copy)
         multiply_h(0)
-        banks1 = transpose_x(1)
+
+        pieces = [transpose_x(1, passes) for passes in ([0], [1], HALVES[1])]
         drop_h(0)
-        banks2 = transpose_x(2)
-        places = transpose_pairs([h_bf[0]])
-        finish_x(1, 0, banks1)
-        finish_x(1, 1, banks1)
-        finish_x(2, 0, banks2)
+        halves = [transpose_x(2, passes) for passes in HALVES]
+        places = transpose_sorted([h_rounded[0]])
+        for piece in pieces:
+            quantize_x(piece)
+        quantize_x(halves[0])
         group_b_vector(0)
-        finish_x(2, 1, banks2)
-        finish_h(0, *places[0])
-        group_b_scalar(0, 1)
+        quantize_x(halves[1])
+        quantize_h(0, places[0])
+        group_b_scalar(0)
         multiply_h(1)
         multiply_h(2)
         drop_h(1)
@@ -390,18 +394,19 @@ def tile_lora_dropout_output_projection_h1_kernel(
         add_bias((0, 0))
         add_bias((1, 0))
         multiply_y((0, 0))
-        places = transpose_pairs([h_bf[1], h_bf[2]])
+
+        places = transpose_sorted([h_rounded[1]]) + transpose_sorted([h_rounded[2]])
         finish_y((0, 0))
-        finish_h(1, *places[0])
-        finish_h(2, *places[1])
-        group_b_scalar(1, 1)
+        quantize_h(1, places[0])
+        quantize_h(2, places[1])
+        group_b_scalar(1)
         round_y((0, 0))
         group_b_vector(1)
+        add_bias((2, 0))
         multiply_y((1, 0))
         finish_y((1, 0))
         round_y((1, 0))
         quantize_b(1)
-        add_bias((2, 0))
         multiply_y((2, 0))
         sort_x(HEAD)
         finish_y((2, 0))
@@ -412,70 +417,83 @@ def tile_lora_dropout_output_projection_h1_kernel(
         round_y((0, 1))
         add_bias((1, 1))
         multiply_y((1, 1))
+        add_bias((2, 1))
 
         final = (TILES - 1, GROUPS - 1)
 
-        def step(h_tile, x_tile, done, last, todo, b_group):
-            lead = 1 if h_tile is not None else 0
-            if x_tile is not None and x_tile + 2 < TILES:
+        def step(h_tile, x_tile, turn, pending, todo):
+            has_h = h_tile is not None
+            has_x = x_tile is not None
+            if has_x and x_tile + 2 < TILES:
                 load_x(x_tile + 2)
                 load_drop(x_tile + 2)
-            if x_tile is not None and x_tile + 1 < TILES:
+            if has_x and x_tile + 1 < TILES:
                 load_res(x_tile + 1)
-            places = transpose_pairs([h_bf[h_tile], y_bf[done[0]]]) if lead else []
-            banks = transpose_x(x_tile) if x_tile is not None else None
-            places = places + transpose_pairs([y_bf[unit] for unit in done[lead:]])
-            finish_y(last)
-            if lead:
-                finish_h(h_tile, *places[0])
-            if b_group is not None:
-                group_b_scalar(b_group, 1)
-                group_b_vector(b_group)
-            add_bias(todo[1])
-            if b_group is not None:
-                quantize_b(b_group)
-            if x_tile is not None:
-                finish_x(x_tile, 0, banks)
-            if x_tile is not None:
-                finish_x(x_tile, 1, banks)
+
+            halves = [transpose_x(x_tile, HALVES[0])] if has_x else []
+            places = transpose_sorted([h_rounded[h_tile], y_rounded[turn[0]]]) if has_h else []
+            if has_x:
+                halves.append(transpose_x(x_tile, HALVES[1]))
+            places = places + transpose_sorted([y_rounded[unit] for unit in (turn[1:] if has_h else turn)])
+
+            if has_h:
+                finish_y(pending)
+                quantize_h(h_tile, places[0])
+                places = places[1:]
+                add_bias(todo[1])
+                for piece in halves:
+                    quantize_x(piece)
+            else:
+                group_b_scalar(GROUPS - 1)
+                group_b_vector(GROUPS - 1)
+                finish_y(pending)
+                quantize_b(GROUPS - 1)
+                for piece in halves:
+                    quantize_x(piece)
+                add_bias(todo[1])
             add_bias(todo[2])
-            finish_planes(done, places[lead:], last)
-            if x_tile is not None and x_tile + 1 < TILES:
+            grouped = [copy_y(place, nc.scalar.copy) for place in places]
+            round_y(pending)
+            for n in range(len(turn)):
+                quantize_y(turn[n], grouped[n])
+            if has_x and x_tile + 1 < TILES:
                 sort_x(x_tile + 1)
+
             for n in range(len(todo) - 1):
                 multiply_y(todo[n])
                 finish_y(todo[n])
                 round_y(todo[n])
                 if n + 3 < len(todo):
                     add_bias(todo[n + 3])
-                if n == 1 and x_tile is not None:
+                if n == 1 and has_x:
                     multiply_h(x_tile)
                     drop_h(x_tile)
             if todo[-1] != final:
                 multiply_y(todo[-1])
                 add_bias((x_tile, 0))
 
-        add_bias((2, 1))
-        step(None, HEAD, [(0, 0), (1, 0), (2, 0), (0, 1)], (1, 1), [(2, 1), (0, 2), (1, 2), (2, 2)], 2)
-        done = [(1, 1), (2, 1), (0, 2), (1, 2)]
+        step(None, HEAD, [(0, 0), (1, 0), (2, 0)], (1, 1), [(2, 1), (0, 2), (1, 2), (2, 2)])
+        turn = [(0, 1), (1, 1), (2, 1), (0, 2), (1, 2)]
         for i in range(HEAD, TILES):
-            step(i, i + 1 if i + 1 < TILES else None, done, (i - 1, 2), [(i, c) for c in range(GROUPS)], None)
-            done = [(i - 1, 2), (i, 0), (i, 1)]
+            step(i, i + 1 if i + 1 < TILES else None, turn, (i - 1, GROUPS - 1), [(i, c) for c in range(GROUPS)])
+            turn = [(i - 1, GROUPS - 1), (i, 0), (i, 1)]
 
-        result = kept("y_final", [P, PASS], F32)
-        rounded = staged("ybf", [P, PASS], BF16, 7)
-        for j in range(4):
+        y_final = kept("y_final", [P, PASS], F32)
+        y_rounded[final] = staged("y_rounded", [P, PASS], BF16, Y_ROUNDED_BUFS)
+        quarter = P // 4
+        for j in range(PASS // P):
             acc = multiply_columns(final, j * P, P)
             part = y_f32[final][:, j * P:(j + 1) * P]
             nc.vector.tensor_tensor(
-                out=sorted_out(rounded[:])[:, :, j * 32:(j + 1) * 32, :], in0=sorted_in(acc[:]), in1=sorted_in(part), op=ADD
+                out=as_sorted(y_rounded[final][:])[:, :, j * quarter:(j + 1) * quarter, :],
+                in0=as_natural(acc[:]), in1=as_natural(part), op=ADD,
             )
-            nc.vector.tensor_tensor(out=result[:, j * P:(j + 1) * P], in0=acc[:], in1=part, op=ADD)
-        nc.sync.dma_start(out=out_0[M - P:M, N - PASS:N], in_=result[:])
-        places = transpose_pairs([y_bf[unit] for unit in done])
-        t = bank([P, 4, P])
-        transpose_pair(t, 0, word_halves(rounded))
-        places.append((t, 0))
-        done.append(final)
-        for n in range(len(done)):
-            quantize_y(done[n], copy_y(*places[n]))
+            nc.vector.tensor_tensor(out=y_final[:, j * P:(j + 1) * P], in0=acc[:], in1=part, op=ADD)
+        nc.sync.dma_start(out=out_0[M - P:M, N - PASS:N], in_=y_final[:])
+
+        turn.append(final)
+        places = [transpose_sorted([y_rounded[unit]])[0] for unit in turn]
+        copies = [nc.scalar.copy, nc.vector.tensor_copy, nc.scalar.copy, nc.scalar.copy]
+        grouped = [copy_y(places[n], copies[n]) for n in range(len(turn))]
+        for n in range(len(turn)):
+            quantize_y(turn[n], grouped[n])

from contextlib import ExitStack

import concourse.mybir as mybir
from concourse.masks import make_identity

M, K, R, N = 1024, 2048, 512, 1536
LORA_SCALE = 2.0
FLOPS = 2 * M * (K * R + K * N + R * N)

F32 = mybir.dt.float32
BF16 = mybir.dt.bfloat16
I32 = mybir.dt.int32
U32 = mybir.dt.uint32
U8 = mybir.dt.uint8
FP8X4 = mybir.dt.float8_e4m3fn_x4
FP4X4 = mybir.dt.float4_e2m1fn_x4
MULT = mybir.AluOpType.mult
ADD = mybir.AluOpType.add

P = 128
PASS = 512
PAIRS = PASS // 2
PASSES = K // PASS
TILES = M // P
GROUPS = N // PASS
BANKS = 8
HALVES = ([0, 1], [2, 3])
HEAD = 3
STORE_BLOCKS = [(0, 3), (3, 6), (6, 8)]
X_SORTED_BUFS = 2
X_GROUPED_BUFS = 3
B_GROUPED_BUFS = 2
H_ROUNDED_BUFS = 3
H_GROUPED_BUFS = 2
Y_BUFS = 11
Y_ROUNDED_BUFS = 7
Y_GROUPED_BUFS = 5


def tile_lora_dropout_output_projection_h1_kernel(
    tc, x, w0_words, w0_scales, a_words, a_scales, drop, b, bias, residual, out_0, out_1, out_2
):
    nc = tc.nc
    with ExitStack() as ctx:
        keep = ctx.enter_context(tc.tile_pool(name="keep", bufs=1))
        stage = ctx.enter_context(tc.tile_pool(name="stage", bufs=2))
        psum = ctx.enter_context(tc.psum_pool(name="psum", bufs=1))
        ctx.enter_context(tc.manual_schedule())

        def kept(name, shape, dtype):
            return keep.tile(shape, dtype, name=name, align_bytes=256 if dtype in (U8, U32) else 64)

        def staged(tag, shape, dtype, bufs):
            return stage.tile(shape, dtype, name=tag, tag=tag, bufs=bufs, align_bytes=64)

        banks_taken = []

        def bank(shape):
            tag = "bank%d" % (len(banks_taken) % BANKS)
            banks_taken.append(tag)
            return psum.tile(shape, F32, name=tag, tag=tag)

        ident = kept("ident", [P, P], F32)
        make_identity(nc, ident[:])

        a_plane = kept("a_plane", [P, PASSES, R], U8)
        w_plane_first = kept("w_plane_first", [P, PASSES, PASS], U8)
        w_plane_rest = kept("w_plane_rest", [P, PASSES, N - PASS], U8)
        for plane in (a_plane, w_plane_first, w_plane_rest):
            nc.vector.memset(plane[:].bitcast(I32), 0)

        x_tile_pairs = {}
        x_pass_pairs = {}
        a_sb = {}
        w_sb = {}
        b_sb = {}
        drop_sb = {}
        res_sb = {}

        def load_scales(plane, rows):
            by_r = rows.rearrange("g (q r) n -> r q g n", r=4)
            for r in range(4):
                nc.sync.dma_start(out=plane[:].bitcast(I32)[r:P:32, :, :], in_=by_r[r])

        def load_x_first():
            for first, end in ((0, 1), (1, 2), (2, 4)):
                t = kept("x0_%d" % first, [P, (end - first) * PASS], BF16)
                nc.sync.dma_start(out=t[:], in_=x[0:P, first * PASS:end * PASS])
                for g in range(first, end):
                    x_pass_pairs[(0, g)] = t[:].bitcast(F32)[:, (g - first) * PAIRS:(g - first + 1) * PAIRS]

        def load_x(i):
            t = kept("x%d" % i, [P, K], BF16)
            nc.sync.dma_start(out=t[:], in_=x[i * P:(i + 1) * P, :])
            x_tile_pairs[i] = t[:].bitcast(F32)
            for g in range(PASSES):
                x_pass_pairs[(i, g)] = x_tile_pairs[i][:, g * PAIRS:(g + 1) * PAIRS]

        def load_a(half):
            t = kept("a%d" % half, [P, 2, 2 * R], U8)
            src = a_words.bitcast(I32)[2 * half:2 * half + 2].rearrange("g p n -> p g n")
            nc.sync.dma_start(out=t[:].bitcast(I32), in_=src)
            for n in range(2):
                a_sb[2 * half + n] = t[:, n, :]

        def load_drop(i):
            t = kept("drop%d" % i, [P, R], BF16)
            nc.sync.dma_start(out=t[:], in_=drop[i * P:(i + 1) * P, :])
            drop_sb[i] = t

        def load_w(c):
            t = kept("w%d" % c, [P, PASSES, 2 * PASS], U8)
            per_group = 2 * PASS // 4
            src = w0_words.bitcast(I32)[:, :, c * per_group:(c + 1) * per_group].rearrange("g p n -> p g n")
            nc.sync.dma_start(out=t[:].bitcast(I32), in_=src)
            w_sb[c] = t

        def load_b(c):
            t = kept("b%d" % c, [P, 4, PASS], BF16)
            nc.sync.dma_start(out=t[:], in_=b[:, c * PASS:(c + 1) * PASS].rearrange("(p t) n -> p t n", t=4))
            b_sb[c] = t

        def load_res_head(c):
            t = kept("res_head%d" % c, [P, HEAD, PASS], BF16)
            src = residual[0:HEAD * P, c * PASS:(c + 1) * PASS].rearrange("(i p) n -> p i n", p=P)
            nc.sync.dma_start(out=t[:], in_=src)
            for i in range(HEAD):
                res_sb[(i, c)] = t[:, i, :]

        def load_res(i):
            t = kept("res%d" % i, [P, N], BF16)
            nc.sync.dma_start(out=t[:], in_=residual[i * P:(i + 1) * P, :])
            for c in range(GROUPS):
                res_sb[(i, c)] = t[:, c * PASS:(c + 1) * PASS]

        load_x_first()
        bias_col = kept("bias_col", [P, GROUPS * 4], BF16)
        nc.sync.dma_start(
            out=bias_col[:].rearrange("p (c t) -> p c t", t=4),
            in_=bias.rearrange("(c p t) -> p c t", p=P, t=4),
        )
        load_scales(a_plane, a_scales.bitcast(I32))
        load_a(0)
        load_a(1)
        load_x(1)
        load_x(2)
        load_drop(0)
        load_b(0)
        load_drop(1)
        load_w(0)
        load_scales(w_plane_first, w0_scales.bitcast(I32)[:, :, 0:PASS // 4])
        load_drop(2)
        load_res_head(0)
        load_b(1)
        load_w(1)
        load_scales(w_plane_rest, w0_scales.bitcast(I32)[:, :, PASS // 4:N // 4])
        load_x(HEAD)
        load_res_head(1)
        load_b(2)
        load_w(2)
        load_drop(HEAD)
        load_res_head(2)
        load_x(HEAD + 1)
        load_drop(HEAD + 1)
        load_res(HEAD)

        def w_plane(g, c):
            if c == 0:
                return w_plane_first[:, g, :]
            return w_plane_rest[:, g, (c - 1) * PASS:c * PASS]

        bias_rows = kept("bias_rows", [P, N], BF16)
        x_sorted = {}
        x_q = {}
        h_bank = {}
        h_rounded = {}
        h_q = {}
        b_grouped = {}
        b_q = {}
        y_bank = {}
        y_f32 = {}
        y_rounded = {}
        y_words = {}
        y_plane = {}
        for first, end in STORE_BLOCKS:
            width = (end - first) * P
            plane = kept("y_plane%d" % first, [P, GROUPS, width], U8)
            for c in range(GROUPS):
                words = kept("y_words%d_%d" % (first, c), [P, width], U32)
                for i in range(first, end):
                    y_words[(i, c)] = (words, first, end)
            for i in range(first, end):
                y_plane[i] = plane

        def as_sorted(ap):
            return ap.rearrange("p (u q e) -> p u q e", u=2, e=2)

        def as_natural(ap):
            return ap.rearrange("p (q u e) -> p u q e", u=2, e=2)

        def transpose_even_odd(dst, slot, even_odd):
            for u in range(2):
                nc.tensor.transpose(dst[:, slot + u, :], even_odd[u], ident[:])

        def transpose_sorted(sources):
            places = []
            for n in range(len(sources)):
                if n % 2 == 0:
                    t = bank([P, 4, P])
                pairs = sources[n][:].bitcast(F32)
                transpose_even_odd(t, 2 * (n % 2), [pairs[:, 0:P], pairs[:, P:2 * P]])
                places.append((t, 2 * (n % 2)))
            return places

        def copy_side_by_side(dst_pairs, src, slot, copy):
            copy(
                out=dst_pairs.rearrange("p (m u) -> p m u", u=2),
                in_=src[:, slot:slot + 2, :].rearrange("p u m -> p m u"),
            )

        def quantize(words, plane, grouped):
            nc.vector.quantize_mx(out=words.bitcast(FP8X4), scales=plane, in_=grouped)

        def sort_x(i):
            t = staged("x_sorted", [P, K // 2], F32, X_SORTED_BUFS)
            nc.scalar.copy(
                out=t[:].rearrange("p (g u q) -> p g u q", u=2, q=P),
                in_=x_tile_pairs[i].rearrange("p (g q u) -> p g u q", u=2, q=P),
            )
            x_sorted[i] = t

        def transpose_x(i, passes):
            t = bank([P, 2 * len(passes), P])
            for n in range(len(passes)):
                g = passes[n]
                if i in x_sorted:
                    even_odd = [x_sorted[i][:, (2 * g + u) * P:(2 * g + u + 1) * P] for u in range(2)]
                else:
                    even_odd = [x_pass_pairs[(i, g)][:, u:PAIRS:2] for u in range(2)]
                transpose_even_odd(t, 2 * n, even_odd)
            return (i, passes, t)

        def quantize_x(piece):
            i, passes, t = piece
            count = len(passes)
            grouped = staged("x_grouped", [P, count * PASS], BF16, X_GROUPED_BUFS)
            nc.scalar.copy(
                out=grouped[:].bitcast(F32).rearrange("p (g m u) -> p g m u", g=count, u=2),
                in_=t[:].rearrange("p (g u) m -> p g m u", u=2),
            )
            words = kept("x_words%d_%d" % (i, passes[0]), [P, count * P], U32)
            plane = kept("x_plane%d_%d" % (i, passes[0]), [P, count * P], U8)
            quantize(words[:], plane[:], grouped[:])
            for n in range(count):
                x_q[(i, passes[n])] = (words[:, n * P:(n + 1) * P], plane[:, n * P:(n + 1) * P])

        def b_views(c, half):
            if c not in b_grouped:
                b_grouped[c] = staged("b_grouped", [P, 4 * PASS], BF16, B_GROUPED_BUFS)
            cols = PASS // 2
            dst = b_grouped[c][:, half * 4 * cols:(half + 1) * 4 * cols].rearrange("p (n j t) -> p n t j", j=4, t=4)
            src = b_sb[c][:, :, half * cols:(half + 1) * cols].rearrange("p t (n j) -> p n t j", j=4)
            return dst, src

        def group_b_vector(c):
            dst, src = b_views(c, 0)
            nc.vector.tensor_scalar(out=dst, in0=src, scalar1=LORA_SCALE, scalar2=None, op0=MULT)

        def group_b_scalar(c):
            dst, src = b_views(c, 1)
            nc.scalar.activation(out=dst, in_=src, func=mybir.ActivationFunctionType.Copy, scale=LORA_SCALE)

        def quantize_b(c):
            words = kept("b_words%d" % c, [P, PASS], U32)
            plane = kept("b_plane%d" % c, [P, PASS], U8)
            quantize(words[:], plane[:], b_grouped[c][:])
            b_q[c] = (words, plane)

        def multiply_h(i):
            acc = bank([P, R])
            for g in range(PASSES):
                words, plane = x_q[(i, g)]
                nc.tensor.matmul_mx(
                    out=acc[:], lhsT=words.bitcast(FP8X4), lhsT_scale=plane,
                    rhs=a_sb[g].bitcast(FP4X4), rhs_scale=a_plane[:, g, :],
                    start=(g == 0), stop=(g == PASSES - 1),
                )
            h_bank[i] = acc

        def drop_h(i):
            t = staged("h_rounded", [P, R], BF16, H_ROUNDED_BUFS)
            nc.vector.tensor_tensor(
                out=as_sorted(t[:]), in0=as_natural(h_bank[i][:]), in1=as_natural(drop_sb[i][:]), op=MULT
            )
            h_rounded[i] = t

        def quantize_h(i, place):
            grouped = staged("h_grouped", [P, R], BF16, H_GROUPED_BUFS)
            copy_side_by_side(grouped[:].bitcast(F32), place[0], place[1], nc.scalar.copy)
            words = kept("h_words%d" % i, [P, P], U32)
            plane = kept("h_plane%d" % i, [P, P], U8)
            quantize(words[:], plane[:], grouped[:])
            h_q[i] = (words, plane)

        def multiply_columns(unit, first, width):
            i, c = unit
            acc = bank([P, width])
            cols = slice(first, first + width)
            for g in range(PASSES):
                words, plane = x_q[(i, g)]
                nc.tensor.matmul_mx(
                    out=acc[:], lhsT=words.bitcast(FP8X4), lhsT_scale=plane,
                    rhs=w_sb[c][:, g, 2 * first:2 * (first + width)].bitcast(FP4X4), rhs_scale=w_plane(g, c)[:, cols],
                    start=(g == 0), stop=False,
                )
            nc.tensor.matmul_mx(
                out=acc[:], lhsT=h_q[i][0][:].bitcast(FP8X4), lhsT_scale=h_q[i][1][:],
                rhs=b_q[c][0][:, cols].bitcast(FP8X4), rhs_scale=b_q[c][1][:, cols],
                start=False, stop=True,
            )
            return acc

        def multiply_y(unit):
            y_bank[unit] = multiply_columns(unit, 0, PASS)

        def add_bias(unit):
            c = unit[1]
            t = staged("y_f32", [P, PASS], F32, Y_BUFS)
            nc.vector.tensor_tensor(out=t[:], in0=res_sb[unit], in1=bias_rows[:, c * PASS:(c + 1) * PASS], op=ADD)
            y_f32[unit] = t

        def finish_y(unit):
            i, c = unit
            t = y_f32[unit]
            nc.vector.tensor_tensor(out=t[:], in0=y_bank[unit][:], in1=t[:], op=ADD)
            nc.sync.dma_start(out=out_0[i * P:(i + 1) * P, c * PASS:(c + 1) * PASS], in_=t[:])

        def round_y(unit):
            t = staged("y_rounded", [P, PASS], BF16, Y_ROUNDED_BUFS)
            nc.scalar.copy(out=as_sorted(t[:]), in_=as_natural(y_f32[unit][:]))
            y_rounded[unit] = t

        def copy_y(place, copy):
            grouped = staged("y_grouped", [P, PASS], BF16, Y_GROUPED_BUFS)
            copy_side_by_side(grouped[:].bitcast(F32), place[0], place[1], copy)
            return grouped

        def quantize_y(unit, grouped):
            i, c = unit
            words, first, end = y_words[unit]
            cols = slice((i - first) * P, (i - first + 1) * P)
            quantize(words[:, cols], y_plane[i][:, c, cols], grouped[:])
            if i == end - 1:
                dst = out_1[c].rearrange("p m t -> p (m t)").bitcast(I32)[:, first * P:end * P]
                nc.sync.dma_start(out=dst, in_=words[:].bitcast(I32))
                if c == GROUPS - 1:
                    queue = nc.scalar if end == TILES else nc.sync
                    rows = out_2.bitcast(I32)[:, :, first * P // 4:end * P // 4]
                    for q in range(4):
                        queue.dma_start(
                            out=rows[:, 4 * q:4 * q + 4, :].rearrange("g r m -> r g m"),
                            in_=y_plane[i][:].bitcast(I32)[32 * q:32 * q + 4, :, :],
                        )

        pieces = [transpose_x(0, [g]) for g in range(PASSES)]
        bias_pairs = bias_col[:].bitcast(F32)
        bias_banks = [bank([P, 4, P]), bank([P, 4, P])]
        for c in range(GROUPS):
            even_odd = [bias_pairs[:, 2 * c + u:2 * c + u + 1].to_broadcast([P, P]) for u in range(2)]
            transpose_even_odd(bias_banks[c // 2], 2 * (c % 2), even_odd)
        for piece in pieces:
            quantize_x(piece)
        for c in range(GROUPS):
            dst = bias_rows[:].bitcast(F32)[:, c * PAIRS:(c + 1) * PAIRS]
            copy_side_by_side(dst, bias_banks[c // 2], 2 * (c % 2), nc.scalar.copy)
        multiply_h(0)

        pieces = [transpose_x(1, passes) for passes in ([0], [1], HALVES[1])]
        drop_h(0)
        halves = [transpose_x(2, passes) for passes in HALVES]
        places = transpose_sorted([h_rounded[0]])
        for piece in pieces:
            quantize_x(piece)
        quantize_x(halves[0])
        group_b_vector(0)
        quantize_x(halves[1])
        quantize_h(0, places[0])
        group_b_scalar(0)
        multiply_h(1)
        multiply_h(2)
        drop_h(1)
        quantize_b(0)
        drop_h(2)
        add_bias((0, 0))
        add_bias((1, 0))
        multiply_y((0, 0))

        places = transpose_sorted([h_rounded[1]]) + transpose_sorted([h_rounded[2]])
        finish_y((0, 0))
        quantize_h(1, places[0])
        quantize_h(2, places[1])
        group_b_scalar(1)
        round_y((0, 0))
        group_b_vector(1)
        add_bias((2, 0))
        multiply_y((1, 0))
        finish_y((1, 0))
        round_y((1, 0))
        quantize_b(1)
        multiply_y((2, 0))
        sort_x(HEAD)
        finish_y((2, 0))
        round_y((2, 0))
        add_bias((0, 1))
        multiply_y((0, 1))
        finish_y((0, 1))
        round_y((0, 1))
        add_bias((1, 1))
        multiply_y((1, 1))
        add_bias((2, 1))

        final = (TILES - 1, GROUPS - 1)

        def step(h_tile, x_tile, turn, pending, todo):
            has_h = h_tile is not None
            has_x = x_tile is not None
            if has_x and x_tile + 2 < TILES:
                load_x(x_tile + 2)
                load_drop(x_tile + 2)
            if has_x and x_tile + 1 < TILES:
                load_res(x_tile + 1)

            halves = [transpose_x(x_tile, HALVES[0])] if has_x else []
            places = transpose_sorted([h_rounded[h_tile], y_rounded[turn[0]]]) if has_h else []
            if has_x:
                halves.append(transpose_x(x_tile, HALVES[1]))
            places = places + transpose_sorted([y_rounded[unit] for unit in (turn[1:] if has_h else turn)])

            if has_h:
                finish_y(pending)
                quantize_h(h_tile, places[0])
                places = places[1:]
                add_bias(todo[1])
                for piece in halves:
                    quantize_x(piece)
            else:
                group_b_scalar(GROUPS - 1)
                group_b_vector(GROUPS - 1)
                finish_y(pending)
                quantize_b(GROUPS - 1)
                for piece in halves:
                    quantize_x(piece)
                add_bias(todo[1])
            add_bias(todo[2])
            grouped = [copy_y(place, nc.scalar.copy) for place in places]
            round_y(pending)
            for n in range(len(turn)):
                quantize_y(turn[n], grouped[n])
            if has_x and x_tile + 1 < TILES:
                sort_x(x_tile + 1)

            for n in range(len(todo) - 1):
                multiply_y(todo[n])
                finish_y(todo[n])
                round_y(todo[n])
                if n + 3 < len(todo):
                    add_bias(todo[n + 3])
                if n == 1 and has_x:
                    multiply_h(x_tile)
                    drop_h(x_tile)
            if todo[-1] != final:
                multiply_y(todo[-1])
                add_bias((x_tile, 0))

        step(None, HEAD, [(0, 0), (1, 0), (2, 0)], (1, 1), [(2, 1), (0, 2), (1, 2), (2, 2)])
        turn = [(0, 1), (1, 1), (2, 1), (0, 2), (1, 2)]
        for i in range(HEAD, TILES):
            step(i, i + 1 if i + 1 < TILES else None, turn, (i - 1, GROUPS - 1), [(i, c) for c in range(GROUPS)])
            turn = [(i - 1, GROUPS - 1), (i, 0), (i, 1)]

        y_final = kept("y_final", [P, PASS], F32)
        y_rounded[final] = staged("y_rounded", [P, PASS], BF16, Y_ROUNDED_BUFS)
        quarter = P // 4
        for j in range(PASS // P):
            acc = multiply_columns(final, j * P, P)
            part = y_f32[final][:, j * P:(j + 1) * P]
            nc.vector.tensor_tensor(
                out=as_sorted(y_rounded[final][:])[:, :, j * quarter:(j + 1) * quarter, :],
                in0=as_natural(acc[:]), in1=as_natural(part), op=ADD,
            )
            nc.vector.tensor_tensor(out=y_final[:, j * P:(j + 1) * P], in0=acc[:], in1=part, op=ADD)
        nc.sync.dma_start(out=out_0[M - P:M, N - PASS:N], in_=y_final[:])

        turn.append(final)
        places = [transpose_sorted([y_rounded[unit]])[0] for unit in turn]
        copies = [nc.scalar.copy, nc.vector.tensor_copy, nc.scalar.copy, nc.scalar.copy]
        grouped = [copy_y(places[n], copies[n]) for n in range(len(turn))]
        for n in range(len(turn)):
            quantize_y(turn[n], grouped[n])
